import numpy as np, ml_dtypes
CORES = [48,51,52,55]
N = 4
BF = ml_dtypes.bfloat16
V, L, A, T = 4096, 256, 2048, 4
H = L // 2; B = V - T * H
def draw0(rng):
    ax = np.clip(np.floor(rng.random((N, 8, 1, V)) * 300 - 22 + 140 * (rng.random((N, 8, 16, V)) - 0.5)), 0, 255).astype(np.int64)
    zp = np.clip(np.floor(rng.random((N, 8, 1, A)) * 170 + 40 + 160 * (rng.random((N, 8, 16, A)) - 0.5)), 0, 255).astype(np.int64)
    p = np.clip(np.floor(rng.random((N, 8, 1, L)) * 130 + 60 + 160 * (rng.random((N, 8, 16, L)) - 0.5)), 0, 255).astype(np.int64)
    near = (rng.random((N, 8, 1, H)) < 0.6) & (rng.random((N, 8, 16, H)) > 0.15)
    p[..., 1::2] = np.where(near, p[..., ::2], p[..., 1::2])
    rt = rng.integers(0, V, (N, 8, 16, A)); ex = rng.integers(0, V, (N, 8, 16, L))
    ex[..., 1::2] = np.where(rng.random((N, 8, 16, H)) < 0.2, ex[:, :, ::-1, ::2], ex[..., 1::2])
    return ax, rt, zp, ex, p, rng.integers(0, 4096, (N, 8, 16)), rng.integers(0, 4096, (N, 8, 16))
def pack(ax, rt, zp, ex, p, wt, km):
    b = lambda a: np.ascontiguousarray(a.reshape(N, 128, -1)).astype(np.float32).astype(BF)
    w = lambda a: np.ascontiguousarray(a.reshape(N, 128, -1)).astype(np.int32)
    return {"ax": b(ax), "rt": w(rt), "zp": b(zp), "ex": w(ex), "p0": b(p), "wt": w(wt), "km": w(km)}
def setup_inputs(rng):
    return pack(*draw0(rng))
def setup_inputs_spread(rng):
    def uneven(n): return np.minimum(np.floor(np.exp2(1 + 7.3 * rng.random((N, 8, 1, n))) * rng.random((N, 8, 16, n))), 255).astype(np.int64)
    ax, zp, p = uneven(V), uneven(A), uneven(L)
    p[..., 1::2] = np.where(rng.random((N, 8, 1, H)) < 0.4, p[..., ::2], p[..., 1::2])
    rt = np.minimum(np.floor(V * rng.random((N, 8, 16, A)) ** (0.5 + 3 * rng.random((N, 8, 1, A)))), V - 1).astype(np.int64)
    ex = np.minimum(np.floor(V * rng.random((N, 8, 16, L)) ** (0.5 + 3 * rng.random((N, 8, 1, L)))), V - 1).astype(np.int64)
    wt = np.minimum(np.floor(np.exp2(12.1 * rng.random((N, 8, 16)))) - 1, 4095).astype(np.int64)
    km = np.minimum(np.floor(np.exp2(12.1 * rng.random((N, 8, 16)))) - 1, 4095).astype(np.int64)
    return pack(ax, rt, zp, ex, p, wt, km)
def setup_inputs_ends(rng):
    den = np.array([0.0, 0.1, 0.25, 0.5, 0.75, 1.0])
    ax = 255 * (rng.random((N, 8, 16, V)) < rng.choice(den, (N, 8, 1, V))); zp = 255 * (rng.random((N, 8, 16, A)) < rng.choice(den, (N, 8, 1, A)))
    p = 255 * (rng.random((N, 8, 16, L)) < rng.choice(np.array([0.0, 0.25, 0.5, 0.75, 0.9, 1.0]), (N, 8, 1, L)))
    p[..., 1::2] = np.where(rng.random((N, 8, 1, H)) < 0.5, p[..., ::2], p[..., 1::2])
    for g, (a, b) in enumerate(((0.0, 0.4), (0.2, 1.0), (0.3, 0.7), (0.4, 0.0), (0.5, 0.3), (0.7, 0.2), (1.0, 0.3), (0.3, 0.5))):
        ax[:, g, :, 0] = 255 * (rng.random((N, 16)) < a); ax[:, g, :, V - 1] = 255 * (rng.random((N, 16)) < b)
    def names(n): return np.where(rng.random((N, 8, 16, n)) < 0.85, (V - 1) * rng.integers(0, 2, (N, 8, 16, n)), rng.integers(0, V, (N, 8, 16, n)))
    rt, ex = names(A), names(L)
    wt = 4095 * rng.integers(0, 2, (N, 8, 16)); km = 4095 * rng.integers(0, 2, (N, 8, 16))
    wt[:, 7] = 4095; wt[:, 5:7, 15] = 4095; wt[:, 0, 0] = 0; wt[:, 0, 1] = 4095
    for m, k in ((0, 0), (1, 4095), (3, 8), (9, 3856), (15, 3841)): km[:, 5:, m] = k
    one = np.zeros(16, np.int64); one[15] = 1
    for i in (0, 1, L - 2, L - 1): p[:, 5:, :, i] = one
    for i in (2, 3, L - 4, L - 3): p[:, 7, :, i] = 255; p[:, 6, :, i] = 0
    p[N - 1, 7, :, L - 2:] = 255
    for h in (3840, 3841, 4095, 4080, 3832): zp[:, 5:, :, (h * A) >> 12] = 255
    zp[:, 6, :, (4080 * A) >> 12] = 0; zp[:, 6, :, (4095 * A) >> 12] = 0; zp[:, 5, :, (4095 * A) >> 12] = 0
    for h in (8, 4088, 24, 264, 136): zp[:, 7, :, (h * A) >> 12] = 0
    zp[:, 6, :, 0] = 255
    return pack(ax, rt, zp, ex, p, wt, km)
def setup_inputs_corners(rng):
    ax, rt, zp, ex, p, wt, km = draw0(rng)
    cnt = rng.integers(0, 17, (N, 8, 1, V)); cnt[..., :17] = np.arange(17)
    hi = ((np.arange(16)[:, None] + rng.integers(0, 16, (N, 8, 1, V))) & 15) < cnt
    ax = np.where(hi, rng.integers(139, 256, ax.shape), rng.integers(0, 111, ax.shape))
    p = rng.integers(111, 140, p.shape); p[..., 1::2] = np.where(rng.random((N, 8, 1, H)) < 0.5, p[..., ::2], p[..., 1::2])
    sets = ((0, 1, 2, 3), (9, 10, 12, 16), (3, 4), (4, 5, 6, 7, 8), (8, 9), tuple(range(17)), (8,), ())
    full = int(rng.integers(0, N))
    for q in range(N):
        for g in range(8):
            s = 0 if q == full else (q + g) & 7
            cand = np.flatnonzero(np.isin(cnt[q, g, 0], np.array(sets[s], np.int64))) if s < 7 else np.array([0, B - 1, B, B + H - 1, B + H, V - 2, V - 1])
            if s == 6: cand = cand[:1]
            rt[q, g] = cand[rng.integers(0, len(cand), (16, A))]
    nm = (rng.integers(0, V, (N, 8, 1, H)) + (2 * rng.integers(0, V // 2, (N, 8, 1, H)) + 1) * np.arange(32)[:, None]) & (V - 1)
    ea, eb = nm[:, :, :16], nm[:, :, 16:]; rep = np.broadcast_to(nm[:, :, :1], ea.shape)
    kd = (np.arange(H)[None, None, None, :] + np.arange(8)[None, :, None, None] + np.arange(N)[:, None, None, None]) % 6
    lone = eb.copy(); lone[:, :, 0] = ea[:, :, 15]
    ex[..., ::2] = np.where(kd >= 4, rep, ea)
    ex[..., 1::2] = np.where(kd == 0, ea, np.where(kd == 1, ea[:, :, ::-1], np.where(kd == 3, lone, np.where(kd == 4, rep, eb))))
    ch = rng.integers(0, 3, (N, 8, 1, A)); ch[:, 1] = 0
    zp = np.take_along_axis(rng.integers(0, 256, (N, 8, 16, 3)), ch, 3)
    km[:, 2] = rng.integers(0, 4096, (N, 1)); km[:, 3, ::2] = 0; km[:, 3, 1::2] = 4095; wt[:, 4] = 0; wt[:, 6, 1:] = 0; wt[:, 6, 0] = 4095
    return pack(ax, rt, zp, ex, p, wt, km)
def setup_inputs_alike(rng):
    ax, rt, zp, ex, p, wt, km = draw0(rng)
    p[:, ::2] = p[:, ::2, :, :1]
    p[:, 1::2] = np.take_along_axis(p[:, 1::2, :, :4], rng.integers(0, 4, (N, 4, 1, L)), 3)
    rt = np.take_along_axis(rt[..., :8], rng.integers(0, 8, (N, 8, 1, A)), 3)
    rt[:, 3] = rng.choice(np.array([0, V - 1, B, B - 1]), (N, 16, A))
    ex[:, ::2] = rng.choice(np.array([0, 5, B - 1, B, B + H, V - 1]), (N, 4, 16, L))
    zp[:, 4:] = np.take_along_axis(zp[:, 4:, :, :16], rng.integers(0, 16, (N, 4, 1, A)), 3)
    wt[:, 5, :14] = rng.integers(3200, 4096, (N, 14)); wt[:, 5, 14] = 256; wt[:, 5, 15] = 1
    aim = np.array([0, 4095, 4075, 4077, 4087])[np.arange(H // 2) % 5]
    big = rng.integers(200, 256, (N, 14, H // 2))
    rest = (4096 + aim - np.sum(wt[:, 5, :14, None] * big, axis=1)) & 8191
    p[:, 5, :14, 2::4] = big; p[:, 5, 14, 2::4] = rest >> 8; p[:, 5, 15, 2::4] = rest & 255; p[:, 5, :, 3::4] = 0
    for k, v in ((5, V - 3), (6, V - 5), (7, V - 7)):
        rt[:, 5, k] = v; ax[:, 5, :, v] = 0; ax[:, 5, :4, v] = 255; ax[:, 5, 14:, v] = 255
    for v, u in ((V - 3, 4075), (V - 5, 4077), (V - 7, 4087), (V - 3, 4095), (V - 3, 4096)): ax[:, 5, :, (((v * u) >> 5) + v) & (V - 1)] = 255
    return pack(ax, rt, zp, ex, p, wt, km)
def check_inputs(d):
    bad = []
    for k, hi in (("ax", 255), ("rt", V - 1), ("zp", 255), ("ex", V - 1), ("p0", 255), ("wt", 4095), ("km", 4095)):
        v = np.asarray(d[k]).astype(np.float64)
        if not (np.min(v) >= 0 and np.max(v) <= hi): bad.append("range of " + k)
        elif np.any(v != np.floor(v)): bad.append("whole numbers of " + k)
    return bad
def pick(x, e):
    n = e.shape[3]
    return np.take_along_axis(x, e.reshape(N, 8, 1, 16 * n), 3).reshape(N, 8, 16, 16, n)
def reference(ax, rt, zp, ex, p0, wt, km):
    x = ax.astype(np.float32).astype(np.int64).reshape(N, 8, 16, V)
    r = np.zeros((N, 8, 16, A + T * L), np.int64); z = np.zeros((N, 8, 16, A + T * L), np.int64)
    r[..., :A] = rt.reshape(N, 8, 16, A); z[..., :A] = zp.astype(np.float32).astype(np.int64).reshape(N, 8, 16, A)
    e0 = ex.astype(np.int64).reshape(N, 8, 16, L); p = p0.astype(np.float32).astype(np.int64).reshape(N, 8, 16, L)
    w = wt.astype(np.int64).reshape(N, 8, 16, 1); k = km.astype(np.int64).reshape(N, 8, 16, 1); odd = np.zeros(N, np.int64)
    for t in range(T):
        n = A + L * t
        u = np.repeat(np.add.reduce(w * p, axis=2)[:, :, ::2] & 4095, 2, axis=2)[:, :, None, :]
        c = (((((u * u) >> 5) & 4095) + ((k * u) & 4095)) & 4095) * n >> 12
        score = np.sum(np.abs(pick(z, c) - p[:, :, :, None, :]), axis=2)
        a = np.minimum.reduce(score * 4096 + c, axis=2) & 4095
        e = np.take_along_axis(r, a[:, :, None, :], 3)
        v = np.sum(pick(x, e) >= p[:, :, :, None, :], axis=2)
        barred = v < 4 + odd[:, None, None, None]
        e2 = (((e * u) >> 5) + e + 77 * t) & (V - 1)
        v2 = np.sum(pick(x, e2) >= p[:, :, :, None, :], axis=2)
        f = np.where(barred, e0, np.where((v < 9) & (v2 >= v), e2, e))
        odd = np.sum(barred, axis=(1, 2, 3)) & 1
        fa, fb = f[..., ::2].copy(), f[..., 1::2].copy()
        same = fa[:, :, :, None, :] == fb[:, :, None, :, :]
        ca, cb = np.any(same, axis=3), np.any(same, axis=2)
        rec = np.maximum.reduce(np.where(ca[:, :, None], pick(x, fa), 0), axis=3)
        new = B + H * t + np.arange(H)
        f[..., ::2] = np.where(ca, new, fa); f[..., 1::2] = np.where(cb, new, fb)
        src = (np.arange(N) - 1 - t % 3) % N
        f, p = f[src], p[src]
        r[..., n:n + L] = f
        if t < T - 1: z[..., n:n + L] = p
        x[..., B + H * t:B + H * t + H] = rec[src]
        p = (p + 255 - np.take_along_axis(x, f[:, :, :1], 3)) >> 1
    return {"yr": r[..., A:].reshape(N, 128, T * L).astype(np.float32), "yp": p.reshape(N, 128, L).astype(np.float32)}

@@ -1,0 +1,549 @@
+from concourse.mybir import AluOpType, ActivationFunctionType
+
+ALU = AluOpType
+ACT = ActivationFunctionType
+ROUNDS, H, A0, NV, REC = 4, 128, 2048, 4096, 3584
+CHUNKS = ((0, 64), (64, 64))
+SCALAR_LANES = (64, 64)
+REP = "GGGGSSSSSSSSVVVV"
+REC_S = (0.5, 0.5)
+Z_S = ((1, 1),)
+MB_S = (1, 1)
+EQ_S = (0, 0)
+
+F32, BF, I32, U16, F16 = "float32", "bfloat16", "int32", "uint16", "float16"
+LOGICAL = {}
+
+
+def declare(dtype, **bufs):
+    for n, w in bufs.items():
+        LOGICAL[n] = ("sbuf", [128, w], dtype)
+
+
+declare(BF, X=4112, Z=3072, pin=256, ones=2048, blk=128, gsp=144, gmin=144, gz=144, ghalf=144, g0b=144, idb=128, nidb=128, nid100=128,
+        prmb=512, bcb=2048, wh=128, wl=128, rmask=1024, p=256, prep=4096)
+declare(F32, R=3072, whf=1, wlf=1, kf=1, cnt=1, bar=1, seg=128, ef=256, uf=128, pm=256, dd=256, yv=256, junk=128)
+declare(I32, rti=2048, exi=256, wti=1, kmi=1, whi=1, wli=1, cnti=1, par=1, ui=128, u=128, uu=128, ku=128, su=128, hs=128, hh=128, pi=256)
+declare(F16, g0=144, nidh=128, idh=128, prm=512, bc=2048, ch=128, k2048=64)
+declare(U16, cq=128)
+for _t in range(ROUNDS):
+    declare(BF, **{"pn%d" % _t: 256, "Q%d" % _t: 128, "QL%d" % _t: 128})
+    declare(F32, **{"F%d" % _t: 256, "nr%d" % _t: 256})
+    declare(U16, **{"LT%d" % _t: 16, "LL%d" % _t: 16})
+for _c, (_j, _p) in enumerate(CHUNKS):
+    _l = 2 * _p
+    for _d, _names in ((BF, (("de", 16 * _p), ("do", 16 * _p), ("zg", 16 * _p), ("ez", 16 * _p), ("c1", 16 * _l), ("c2", 16 * _l), ("xg", 16 * _l),
+                             ("mb", _l), ("r1", _l), ("g1c", _l), ("eq", 16 * _p), ("cm", _l), ("xr", 16 * _p), ("qs", 16 * _p))),
+                       (F32, (("tr", _l), ("sg", _l), ("e", _l), ("em", _l), ("t1", _l), ("base", _l), ("ma", _l), ("rt1", _p))),
+                       (I32, (("mk", _l), ("ai", _l // 16), ("nn", _l), ("e2", _l))),
+                       (F16, (("ah", _l // 16), ("f", _l), ("fh", _l))),
+                       (U16, (("au", _l // 16), ("eu", _l), ("e2u", _l), ("ro", _p)))):
+        declare(_d, **{"%s_%d" % (n, _c): w for n, w in _names})
+OWN = {"X", "Z", "R", "rti", "exi", "pin", "wti", "kmi"} | {"%s%d" % (n, t) for n in ("pn", "F", "Q", "QL", "LT", "LL") for t in range(ROUNDS)}
+SCRATCH, PLACE = {}, {}
+for _n, (_w, _s, _d) in LOGICAL.items():
+    if _n in OWN:
+        SCRATCH[_n], PLACE[_n] = (_w, _s, _d), (_n, 0)
+    else:
+        _k = "pool_" + _d
+        _o = SCRATCH.get(_k, (0, [128, 0]))[1][1]
+        PLACE[_n] = (_k, _o)
+        SCRATCH[_k] = ("sbuf", [128, _o + (_s[1] + 31) // 32 * 32], _d)
+for _b in range(8):
+    LOGICAL["B%d" % _b] = SCRATCH["B%d" % _b] = ("psum", [128, 512], F32)
+    PLACE["B%d" % _b] = ("B%d" % _b, 0)
+LOADS = ("p0", "wt", "km", "zp", "ax", "rt", "ex")
+KINDS = ("p", "F", "L", "Q")
+SEMAPHORES = (["v", "s", "t", "gp", "out"] + ["ld_" + n for n in LOADS]
+              + ["l%s%d" % (k, t) for k in KINDS for t in range(ROUNDS)] + ["a%s%d" % (k, t) for k in KINDS for t in range(ROUNDS)])
+WIDTH = {n: s[1][1] for n, s in LOGICAL.items()}
+PSUM = {n for n, s in LOGICAL.items() if s[0] == "psum"}
+TWO = {n for n, s in LOGICAL.items() if s[2] in (BF, F16, U16)}
+CYC, GATHER = 1.0e-3, 1.55
+
+
+def A(name, lo=0, hi=None, st=1):
+    return (name, lo, WIDTH[name] if hi is None else hi, st)
+
+
+def Ind(win, off):
+    return ("@", win, off)
+
+
+def size(a):
+    return 16 * size(a[2]) if a[0] == "@" else (a[2] - a[1] + a[3] - 1) // a[3]
+
+
+def ap(T, a):
+    if a[0] == "@":
+        return ap(T, a[1]).indirect(ap(T, a[2]))
+    name, o = PLACE[a[0]]
+    if a[3] == 1:
+        return T[name][:, o + a[1]:o + a[2]]
+    return T[name][:, o + a[1]:o + a[2]:a[3]]
+
+
+def flat(aps):
+    out = []
+    for a in aps:
+        if isinstance(a, tuple):
+            out += [a[1], a[2]] if a[0] == "@" else [a]
+    return out
+
+
+def build():
+    ops = []
+
+    def add(q, cost, outs, ins, fn, **kw):
+        op = dict(q=q, cost=cost, outs=flat(outs), ins=flat(ins), fn=fn, **kw)
+        ops.append(op)
+        return op
+
+    def vcost(aps, mode):
+        n = size(aps[0])
+        if any(a[0] == "@" for a in aps):
+            return 0.06 + n * GATHER * CYC
+        per = 1.0
+        if mode == "tt":
+            per = 1.0 if any(a[0] in PSUM for a in aps[1:]) else 2.0
+        elif all(a[0] in TWO for a in aps):
+            per = 0.5
+        return 0.06 + max(64, n * per) * CYC
+
+    def tt(out, a, b, op):
+        add("V", vcost((out, a, b), "tt"), [out], [a, b], lambda c: c["V"].tensor_tensor(ap(c["T"], out), ap(c["T"], a), ap(c["T"], b), op))
+
+    def ts(out, a, s1, op0, s2=None, op1=None):
+        def fn(c):
+            x1 = ap(c["T"], s1) if isinstance(s1, tuple) else s1
+            if op1 is None:
+                return c["V"].tensor_scalar(ap(c["T"], out), ap(c["T"], a), x1, None, op0)
+            return c["V"].tensor_scalar(ap(c["T"], out), ap(c["T"], a), x1, s2, op0, op1)
+        add("V", vcost((out, a), "ts"), [out], [a, s1], fn)
+
+    def cp(out, a):
+        add("V", vcost((out, a), "ts"), [out], [a], lambda c: c["V"].tensor_copy(ap(c["T"], out), ap(c["T"], a)))
+
+    def fill(out, val):
+        add("V", 0.06 + size(out) * CYC, [out], [], lambda c: c["V"].memset(ap(c["T"], out), val))
+
+    def scan(out, d0, d1, op0, op1):
+        add("V", vcost((out, d0, d1), "ts"), [out], [d0, d1],
+            lambda c: c["V"].tensor_tensor_scan(ap(c["T"], out), ap(c["T"], d0), ap(c["T"], d1), 0.0, op0, op1))
+
+    def vtr(out, a):
+        add("V", vcost((out, a), "ts"), [out], [a], lambda c: c["V"].transpose(ap(c["T"], out), ap(c["T"], a)))
+
+    def act(out, a, func=None, bias=0.0, scale=1.0, accum=None):
+        func = ACT.Identity if func is None else func
+        n = size(out)
+
+        def fn(c):
+            x = ap(c["T"], accum) if accum is not None else None
+            b = ap(c["T"], bias) if isinstance(bias, tuple) else bias
+            return c["S"].activation(ap(c["T"], out), ap(c["T"], a), func, bias=b, scale=scale, accum_out=x)
+        add("S", 0.08 + n * CYC * (GATHER if a[0] == "@" else 1.0), [out] + ([accum] if accum is not None else []), [a, bias], fn)
+
+    def mm(items):
+        def fn(c):
+            m = None
+            for o, l, r, s, e in items:
+                m = c["P"].matmul(ap(c["T"], o), ap(c["T"], l), ap(c["T"], r), s, e)
+            return m
+        outs, ins = [], []
+        for o, l, r, s, e in items:
+            for x, d in ((o, outs), (l, ins), (r, ins)):
+                if x not in d:
+                    d.append(x)
+        add("P", sum(max(64, size(i[2])) for i in items) * 0.5e-3 + 0.02, outs, ins, fn)
+
+    def aff(out, a, pattern, cmp, base, cm):
+        add("G", 0.2 + 2 * size(out) * CYC, [out], [a], lambda c: c["g"].affine_select(ap(c["T"], out), ap(c["T"], a), pattern, cmp, 0.0, base, cm), sem="gp")
+
+    def iota(out, pattern, base):
+        add("G", 0.15 + 2 * size(out) * CYC, [out], [], lambda c: c["g"].iota(ap(c["T"], out), pattern, base, 0, allow_small_or_imprecise_dtypes=True), sem="gp")
+
+    def load(out, name):
+        add("Y", 0.15, [out], [], lambda c: c["g"].sync.dma_start(ap(c["T"], out), c["T"][name][:]), sem="ld_" + name, inc=16, lat=2.0 + size(out) / 2000.0)
+
+    def store(name, lo, hi, a):
+        add("Y", 0.15, [], [a], lambda c: c["g"].sync.dma_start(c["T"][name][:, lo:hi], ap(c["T"], a)), sem="out", inc=16, lat=2.0)
+
+    def send(kind, t, dst, src):
+        def fn(c):
+            to = c["T"].cores[(c["rank"] + 1 + t % 3) % len(c["T"].cores)]
+            topo = c["topo"]
+            rid, pid, _ = topo.addr(to)
+            c["g"].remote_dma(ap(c["T"], dst), ap(c["T"], src), c["T"].sem["a%s%d" % (kind, t)], c["T"].sem["l%s%d" % (kind, t)],
+                              pid, rid, topo.mask(c["core"], to))
+        s = add("G", 0.2, [], [src], fn, sem="l%s%d" % (kind, t), inc=16, own=True, lat=2.0)
+        add("R", 0.0, [dst], [], None, sem="a%s%d" % (kind, t), inc=16, after=s, lat=2.2)
+
+    def route(tab, x):
+        return A(tab, 15 - x, 143 - x)
+
+    load(A("pin"), "p0"); load(A("wti"), "wt"); load(A("kmi"), "km")
+    load(A("Z", 0, A0), "zp"); load(A("X", 0, NV), "ax"); load(A("rti"), "rt"); load(A("exi"), "ex")
+    fill(A("ones", 0, 128), 1.0)
+    aff(A("blk"), A("ones", 0, 128), [[-16, 8], [0, 16]], ALU.is_ge, 0, 1)
+    aff(A("blk"), A("blk"), [[16, 8], [0, 16]], ALU.is_ge, 15, -1)
+    for c, (j0, P) in enumerate(CHUNKS):
+        for par in range(2):
+            cp(A("p", 2 * j0 + par * P, 2 * j0 + par * P + P), A("pin", 2 * j0 + par, 2 * j0 + 2 * P, 2))
+    ts(A("whi"), A("wti"), 6, ALU.logical_shift_right)
+    ts(A("wli"), A("wti"), 63, ALU.bitwise_and)
+    ts(A("whf"), A("whi"), 64.0, ALU.mult)
+    cp(A("wlf"), A("wli"))
+    ts(A("wh"), A("blk"), A("whf"), ALU.mult)
+    ts(A("wl"), A("blk"), A("wlf"), ALU.mult)
+    ts(A("kf"), A("kmi"), 4096.0, ALU.subtract)
+    send("p", 0, A("Z", A0, A0 + 256), A("pin"))
+    fill(A("gsp"), 0.0)
+    aff(A("gsp", 15, 143, 16), A("ones", 0, 8), [[-16, 8]], ALU.is_ge, 0, 1)
+    aff(A("gsp", 15, 143, 16), A("gsp", 15, 143, 16), [[16, 8]], ALU.is_ge, 15, -1)
+    act(A("gmin"), A("gsp"), scale=-8192.0)
+    act(A("gz"), A("gsp"), scale=4096.0)
+    act(A("ghalf"), A("gsp"), scale=0.5)
+    fill(A("seg"), 0.0)
+    fill(A("seg", 0, 128, 16), 1e9)
+    for qh in range(2):
+        for gp in range(2):
+            k = 128 * (2 * qh + gp)
+            aff(A("prmb", k, k + 128), A("ones", 0, 128), [[-32, 4], [-1000, 2], [-1, 16]], ALU.is_equal, 1000 * gp - 16 * qh, 1)
+    cp(A("prm"), A("prmb"))
+    aff(A("idb"), A("ones", 0, 128), [[-1, 128]], ALU.is_equal, 0, 1)
+    act(A("nidb"), A("idb"), scale=-1.0)
+    act(A("nid100"), A("idb"), scale=-100.0)
+    ts(A("nidh"), A("idb"), -1.0, ALU.mult)
+    cp(A("idh"), A("idb"))
+    ts(A("k2048"), A("ones", 0, 64), 2048.0, ALU.mult)
+    fill(A("bar"), 3.5)
+    fill(A("ones", 128, 2048), 1.0)
+    aff(A("bcb"), A("ones"), [[-1, 16], [-16, 8], [0, 16]], ALU.is_equal, 0, 1)
+    fill(A("X", NV, NV + 16), 0.0)
+    fill(A("rmask"), 1.0)
+    fill(A("rmask", 0, 1024, 16), 0.0)
+    fill(A("g0b"), 0.0)
+    aff(A("g0b", 15, 143, 16), A("ones", 0, 8), [[-16, 8]], ALU.is_equal, 0, 1)
+    for k in range(0, 2048, 512):
+        cp(A("bc", k, k + 512), A("bcb", k, k + 512))
+    cp(A("g0"), A("g0b"))
+    for t in range(ROUNDS):
+        for c, (j0, P) in enumerate(CHUNKS):
+            iota(A("nr%d" % t, 2 * j0, 2 * j0 + 2 * P), [[0, 2], [1, P]], REC - 2048 + H * t + j0)
+    for k in range(0, A0, 512):
+        cp(A("R", k, k + 512), A("rti", k, k + 512))
+    for c, (j0, P) in enumerate(CHUNKS):
+        for par in range(2):
+            cp(A("ef", 2 * j0 + par * P, 2 * j0 + par * P + P), A("exi", 2 * j0 + par, 2 * j0 + 2 * P, 2))
+
+    for t in range(ROUNDS):
+        n = A0 + 256 * t
+        NC = len(CHUNKS)
+        if t > 0:
+            for c, (j0, P) in enumerate(CHUNKS):
+                for par in range(2):
+                    aff(A("pn%d" % t, 2 * j0 + par, 2 * j0 + 2 * P, 2), A("p", 2 * j0 + par * P, 2 * j0 + par * P + P), [[0, P]], ALU.is_ge, 0, 0)
+            send("p", t, A("Z", n, n + 256), A("pn%d" % t))
+        for c, (j0, P) in enumerate(CHUNKS):
+            mm([(A("B0", j0, j0 + P), A("wh"), A("p", 2 * j0, 2 * j0 + P), True, False),
+                (A("B0", j0, j0 + P), A("wl"), A("p", 2 * j0, 2 * j0 + P), False, True)])
+        cp(A("ui"), A("B0", 0, 128))
+        ts(A("u"), A("ui"), 4095, ALU.bitwise_and)
+        tt(A("uu"), A("u"), A("u"), ALU.mult)
+        ts(A("ku"), A("u"), A("kf"), ALU.mult)
+        ts(A("su"), A("uu"), 5, ALU.logical_shift_right)
+        tt(A("hs"), A("su"), A("ku"), ALU.add)
+        ts(A("hh"), A("hs"), 4095, ALU.bitwise_and)
+        ts(A("cq"), A("hh"), (8 + t) / 16.0, ALU.mult, -15.0 / 32, ALU.add)
+        for k in range(16):
+            if REP[k] == "S":
+                act(A("prep", k, 4096, 16), A("p"))
+            elif REP[k] == "G":
+                aff(A("prep", k, 4096, 16), A("p"), [[0, 256]], ALU.is_ge, 0, 0)
+            else:
+                cp(A("prep", k, 4096, 16), A("p"))
+        ts(A("ch"), A("cq"), 2048.0, ALU.subtract)
+        cp(A("uf"), A("u"))
+        for c, (j0, P) in enumerate(CHUNKS):
+            for par, d in ((0, "de_%d" % c), (1, "do_%d" % c)):
+                b = 16 * (2 * j0 + par * P)
+                if (c, par) not in Z_S:
+                    tt(A(d), Ind(A("Z", 0, n), A("cq", j0, j0 + P)), A("prep", b, b + 16 * P), ALU.min)
+            act(A("zg_%d" % c), Ind(A("Z", 0, n), A("cq", j0, j0 + P)))
+        for c, par in Z_S:
+            j0, P = CHUNKS[c]
+            b = 16 * (2 * j0 + par * P)
+            for i, k in enumerate(range(0, 16 * P, 512)):
+                sb = ("B7", "B6")[i % 2]
+                mm([(A(sb), A("idb"), A("zg_%d" % c, k, k + 512), True, False), (A(sb), A("nidb"), A("prep", b + k, b + k + 512), False, True)])
+                act(A("%s_%d" % (("de", "do")[par], c), k, k + 512), A(sb), ACT.Abs)
+        for c, (j0, P) in enumerate(CHUNKS):
+            L, bk, tb, cs = 2 * P, "B%d" % (1 + c % 2), "B%d" % (3 + c % 2), "_%d" % c
+            for par, d in ((0, "de"), (1, "do")):
+                o = A(bk, par * P, par * P + P)
+                mm([(o, A("idh"), A("k2048", 0, P), True, False), (o, A("idh"), A("ch", j0, j0 + P), False, False)]
+                   + [(o, route("gz", m), A("zg" + cs, m, 16 * P, 16), False, False) for m in range(16) if (c, par) not in Z_S])
+                mm([(o, route("gz" if (c, par) in Z_S else "gmin", m), A(d + cs, m, 16 * P, 16), False, m == 15) for m in range(16)])
+            vtr(A("tr" + cs), A(bk, 0, L))
+            scan(A("mk" + cs), A("seg", 0, L), A("tr" + cs), ALU.add, ALU.min)
+            ts(A("ai" + cs), A("mk" + cs, 15, L, 16), 4095, ALU.bitwise_and)
+            ts(A("ah" + cs), A("ai" + cs), 2048.0, ALU.subtract)
+            q0 = 128 + 2 * j0 // 16
+            items = []
+            for qh in range(2):
+                for gp in range(2):
+                    k = 128 * (2 * qh + gp)
+                    items.append((A("B0", q0 + qh, q0 + L // 16, 2), A("prm", k, k + 128), A("ah" + cs, gp, L // 16, 2), gp == 0, gp == 1))
+            mm(items)
+            ts(A("au" + cs), A("B0", q0, q0 + L // 16), 2048.0, ALU.add)
+            cp(A("eu" + cs), Ind(A("R", 0, n), A("au" + cs)))
+            act(A("e" + cs), Ind(A("R", 0, n), A("au" + cs)))
+            for par in range(2):
+                act(A(tb, par * P, par * P + P), A("uf", j0, j0 + P))
+            act(A(tb, 128, 128 + L), A("e" + cs), bias=2464.0 * t - 131072.0, scale=32.0)
+            act(A(tb, 256, 256 + L), A("e" + cs))
+            tt(A("t1" + cs), A("e" + cs), A(tb, 0, L), ALU.mult)
+            tt(A("nn" + cs), A("t1" + cs), A(tb, 128, 128 + L), ALU.add)
+            ts(A("e2" + cs), A("nn" + cs), 5, ALU.arith_shift_right, 4095, ALU.bitwise_and)
+            cp(A("e2u" + cs), A("e2" + cs))
+        for c, (j0, P) in enumerate(CHUNKS):
+            L, bk, tb, cs = 2 * P, "B%d" % (1 + c % 2), "B%d" % (3 + c % 2), "_%d" % c
+            b = 32 * j0
+            for h in range(2):
+                tt(A("c1" + cs, 16 * P * h, 16 * P * h + 16 * P), Ind(A("X", 0, NV), A("eu" + cs, h * P, h * P + P)),
+                   A("prep", b + 16 * P * h, b + 16 * P * h + 16 * P), ALU.is_ge)
+            act(A("em" + cs), A("e" + cs), bias=-2048.0)
+            tt(A(tb, 384, 384 + L), A("ef", 2 * j0, 2 * j0 + L), A(tb, 256, 256 + L), ALU.subtract)
+            tt(A(tb, 0, L), A("e2" + cs), A(tb, 256, 256 + L), ALU.subtract)
+            ns = SCALAR_LANES[c]
+            for i, l0 in enumerate(range(0, ns, 32)):
+                sb = ("B7", "B6" if c == 0 else "B0")[i % 2]
+                x = A("xg" + cs, 16 * l0, 16 * (l0 + 32))
+                act(x, Ind(A("X", 0, NV), A("e2u" + cs, l0, l0 + 32)))
+                mm([(A(sb), A("idb"), x, True, False),
+                    (A(sb), A("nidb"), A("prep", b + 16 * l0, b + 16 * (l0 + 32)), False, True)])
+                act(A("c2" + cs, 16 * l0, 16 * (l0 + 32)), A(sb), ACT.Sign, bias=0.5)
+            for l0 in range(ns, L, 64):
+                hi = min(l0 + 64, L)
+                tt(A("c2" + cs, 16 * l0, 16 * hi), Ind(A("X", 0, NV), A("e2u" + cs, l0, hi)), A("prep", b + 16 * l0, b + 16 * hi), ALU.is_ge)
+        for c, (j0, P) in enumerate(CHUNKS):
+            L, bk, tb, cs = 2 * P, "B%d" % (1 + c % 2), "B%d" % (3 + c % 2), "_%d" % c
+            ns = SCALAR_LANES[c]
+            for h in range(2):
+                mm([(A(bk, 128 + h * P, 128 + h * P + P), route("gsp", k), A("c1" + cs, 16 * P * h + k, 16 * P * h + 16 * P, 16), k == 0, k == 15) for k in range(16)])
+            if MB_S[c]:
+                act(A("sg" + cs), A(bk, 128, 128 + L), ACT.Sign, bias=A("bar"), scale=-1.0)
+                act(A("mb" + cs), A("sg" + cs), ACT.Relu)
+            else:
+                ts(A("mb" + cs), A(bk, 128, 128 + L), A("bar"), ALU.is_lt)
+            act(A("r1" + cs), A(bk, 128, 128 + L), ACT.Relu, bias=-800.0, scale=100.0)
+            if ns > 0:
+                act(A("g1c" + cs, 0, ns), A(bk, 128, 128 + ns), bias=-8.0)
+            if ns < L:
+                act(A("g1c" + cs, ns, L), A(bk, 128 + ns, 128 + L))
+            tt(A(tb, 128, 128 + L), A("mb" + cs), A(tb, 384, 384 + L), ALU.mult)
+            tt(A("base" + cs), A(tb, 128, 128 + L), A("em" + cs), ALU.add)
+            for lo, hi, tab in [(0, ns, "ghalf")] * (ns > 0) + [(l0, min(l0 + 64, L), "gsp") for l0 in range(ns, L, 64)]:
+                o = A(bk, 256 + lo, 256 + hi)
+                mm([(o, A("nid100"), A("mb" + cs, lo, hi), True, False), (o, A("nidb"), A("r1" + cs, lo, hi), False, False),
+                    (o, A("nidb"), A("g1c" + cs, lo, hi), False, False)]
+                   + [(o, route(tab, k), A("c2" + cs, 16 * lo + k, 16 * hi, 16), False, k == 15) for k in range(16)])
+            ts(A("ma" + cs), A(bk, 256, 256 + L), 0.0, ALU.is_ge)
+            tt(A(tb, 256, 256 + L), A("ma" + cs), A(tb, 0, L), ALU.mult)
+            tt(A("f" + cs), A(tb, 256, 256 + L), A("base" + cs), ALU.add)
+            tt(A(tb, 0, L), A("nr%d" % t, 2 * j0, 2 * j0 + L), A("f" + cs), ALU.subtract)
+            for h in range(2):
+                eb = "B%d" % (5 + h)
+                items = []
+                for k in range(8):
+                    o = A(eb, k * P, k * P + P)
+                    items.append((o, A("nidh"), A("f" + cs, 0, P), True, False))
+                    items.append((o, A("bc", 128 * (8 * h + k), 128 * (8 * h + k) + 128), A("f" + cs, P, L), False, True))
+                mm(items)
+                x = A("eq" + cs, 8 * P * h, 8 * P * h + 8 * P)
+                if EQ_S[c]:
+                    y = A("ez" + cs, 8 * P * h, 8 * P * h + 8 * P)
+                    act(y, A(eb, 0, 8 * P), ACT.Abs)
+                    act(x, y, ACT.Relu, bias=1.0, scale=-1.0)
+                else:
+                    ts(x, A(eb, 0, 8 * P), 0.0, ALU.is_equal)
+            for par in range(2):
+                mm([(A(bk, 384 + par * P, 384 + par * P + P), route("gsp", k) if par else A("idb"), A("eq" + cs, k * P, k * P + P), k == 0, k == 15) for k in range(16)])
+            act(A(tb, 384, 384 + P), A(bk, 384, 384 + P), bias=2048.0, scale=-8192.0)
+            act(A("cm" + cs), A(bk, 384, 384 + L), ACT.Sign)
+            tt(A("rt1" + cs), A(tb, 384, 384 + P), A("f" + cs, 0, P), ALU.max)
+            ts(A("ro" + cs), A("rt1" + cs), 2048.0, ALU.add)
+            ps = int(P * REC_S[c]) // 16 * 16
+            if ps:
+                act(A("xr" + cs, 0, 16 * ps), Ind(A("X"), A("ro" + cs, 0, ps)))
+            if ps < P:
+                cp(A("xr" + cs, 16 * ps, 16 * P), Ind(A("X"), A("ro" + cs, ps, P)))
+            tt(A(tb, 128, 128 + L), A("cm" + cs), A(tb, 0, L), ALU.mult)
+            tt(A("fh" + cs), A(tb, 128, 128 + L), A("f" + cs), ALU.add)
+            for par in range(2):
+                mm([(A("B0", 256 + 2 * j0 + par, 256 + 2 * j0 + L, 2), A("nidh"), A("fh" + cs, par * P, par * P + P), True, True)])
+            act(A("F%d" % t, 2 * j0, 2 * j0 + L), A("B0", 256 + 2 * j0, 256 + 2 * j0 + L), bias=2048.0, scale=-1.0)
+            q0 = 160 + 2 * j0 // 16
+            mm([(A("B0", q0, q0 + L // 16), route("g0", x), A("fh" + cs, x, L, 16), x == 0, x == 15) for x in range(16)])
+            ts(A("LT%d" % t, 2 * j0 // 16, 2 * j0 // 16 + L // 16), A("B0", q0, q0 + L // 16), 2048.0, ALU.add)
+            scan(A("qs" + cs), A("rmask", 0, 16 * P), A("xr" + cs), ALU.mult, ALU.max)
+            cp(A("Q%d" % t, j0, j0 + P), A("qs" + cs, 15, 16 * P, 16))
+        send("F", t, A("R", n, n + 256), A("F%d" % t))
+        send("L", t, A("LL%d" % t), A("LT%d" % t))
+        send("Q", t, A("QL%d" % t), A("Q%d" % t))
+        if t < ROUNDS - 1:
+            mm([(A("B7", 0, 2 * P), A("ones", 0, 128), A("mb_%d" % c), c == 0, c == NC - 1) for c, (j0, P) in enumerate(CHUNKS)])
+            P0 = CHUNKS[0][1]
+            act(A("junk", 0, 2 * P0), A("B7", 0, 2 * P0), accum=A("cnt"))
+            cp(A("cnti"), A("cnt"))
+            ts(A("par"), A("cnti"), 1, ALU.bitwise_and)
+            ts(A("bar"), A("par"), 3.5, ALU.add)
+        store("yr", 256 * t, 256 * t + 256, A("R", n, n + 256))
+        for c, (j0, P) in enumerate(CHUNKS):
+            for par in range(2):
+                act(A("pm", 2 * j0 + par * P, 2 * j0 + par * P + P), A("Z", n + 2 * j0 + par, n + 2 * j0 + 2 * P, 2), bias=255.0)
+        cp(A("X", REC + H * t, REC + H * t + H), A("QL%d" % t))
+        tt(A("dd"), Ind(A("X", 0, NV), A("LL%d" % t)), A("pm"), ALU.subtract)
+        ts(A("pi"), A("dd"), -0.5, ALU.mult, -0.25, ALU.add)
+        if t < ROUNDS - 1:
+            cp(A("p"), A("pi"))
+        else:
+            for c, (j0, P) in enumerate(CHUNKS):
+                for par in range(2):
+                    cp(A("yv", 2 * j0 + par, 2 * j0 + 2 * P, 2), A("pi", 2 * j0 + par * P, 2 * j0 + par * P + P))
+            store("yp", 0, 256, A("yv"))
+    return ops
+
+
+def overlap(a, b):
+    if a[1] >= b[2] or b[1] >= a[2]:
+        return False
+    return not (a[3] == b[3] and a[3] > 1 and (a[1] - b[1]) % a[3])
+
+
+def dependencies(ops):
+    hist = {}
+    for i, op in enumerate(ops):
+        op["i"] = i
+        deps = {}
+        acc = [(a, False) for a in op["ins"]] + [(a, True) for a in op["outs"]]
+        for a, wr in acc:
+            bank = a[0] in PSUM
+            for j, b, bw in hist.setdefault(a[0], []):
+                same = ops[j]["q"] == op["q"]
+                if (wr or bw) and overlap(a, b):
+                    deps[j] = deps.get(j, False) or not same or (bw and not wr)
+                elif bank and not same:
+                    deps[j] = True
+                elif bank and op["q"] == "P":
+                    deps[j] = deps.get(j, False)
+        for a, wr in acc:
+            h = hist[a[0]]
+            if a[0] in PSUM:
+                h[:] = [e for e in h if e[0] >= i - 400]
+            elif wr and a[3] == 1:
+                h[:] = [e for e in h if not (e[0] != i and e[1][1] >= a[1] and e[1][2] <= a[2])]
+            h.append((i, a, wr))
+        op["deps"] = deps
+
+
+def schedule(ops, slack=0.0, wake=0.12):
+    n = len(ops)
+    succ = [[] for _ in range(n)]
+    npred = [0] * n
+    for i, op in enumerate(ops):
+        op["preds"] = set(op["deps"]) | ({op["after"]["i"]} if "after" in op else set())
+        npred[i] = len(op["preds"])
+        for j in op["preds"]:
+            succ[j].append(i)
+    prio = [0.0] * n
+    for i in range(n - 1, -1, -1):
+        b = max([prio[k] + (0.0 if ops[k]["q"] == ops[i]["q"] else wake) for k in succ[i]] + [0.0])
+        prio[i] = b + ops[i]["cost"] + ops[i].get("lat", 0.0)
+    free, count, done = {}, {}, [0.0] * n
+    ready = {i for i in range(n) if npred[i] == 0}
+    while ready:
+        best = {}
+        for i in sorted(ready):
+            q = ops[i]["q"]
+            s = free.get(q, 0.0) if q != "R" else 0.0
+            for j in ops[i]["preds"]:
+                s = max(s, done[j] + (wake if ops[j]["q"] != q else 0.02))
+            best.setdefault(q, []).append((s, i))
+        pick = None
+        for q, lst in sorted(best.items()):
+            m = min(s for s, _ in lst)
+            s, i = max(((s, i) for s, i in lst if s <= m + slack), key=lambda e: (prio[e[1]], -e[1]))
+            if pick is None or (s, -prio[i]) < pick[:2]:
+                pick = (s, -prio[i], i, q)
+        s, _, i, q = pick
+        ready.remove(i)
+        free[q] = s + ops[i]["cost"]
+        done[i] = s + ops[i]["cost"] + ops[i].get("lat", 0.0)
+        count[q] = count.get(q, 0) + 1
+        ops[i]["pos"] = (s, count[q])
+        for k in succ[i]:
+            npred[k] -= 1
+            if npred[k] == 0:
+                ready.add(k)
+
+
+PLAN = {}
+
+
+def plan():
+    if not PLAN:
+        ops = build()
+        dependencies(ops)
+        schedule(ops)
+        PLAN["ops"], PLAN["seq"] = ops, sorted(range(len(ops)), key=lambda i: ops[i]["pos"])
+    return PLAN["ops"], PLAN["seq"]
+
+
+def rank_program(g, core, T, topo):
+    rank = T.rank_of(core)
+    if rank is None:
+        return
+    ops, seq = plan()
+    ctx = dict(g=g, V=g.vector, S=g.scalar, P=g.tensor, T=T, topo=topo, core=core, rank=rank)
+    queue = {"V": g.vector, "S": g.scalar, "P": g.tensor, "G": g, "Y": g.sync}
+    default = {"V": "v", "S": "s", "P": "t"}
+    total, val, known, clock = {}, {}, {q: {} for q in queue}, {}
+    for i in seq:
+        op = ops[i]
+        q = op["q"]
+        name = op.get("sem") or default[q]
+        inc = op.get("inc", 1)
+        if q == "R":
+            total[name] = total.get(name, 0) + inc
+            val[i], clock[i] = (name, total[name]), {name: total[name]}
+            continue
+        kn = known[q]
+        hard = [j for j, h in op["deps"].items() if h]
+        need = {}
+        for j in hard:
+            s, v = val[j]
+            if kn.get(s, 0) < v:
+                need[s] = max(need.get(s, 0), v)
+        for j in sorted(hard, key=lambda j: -ops[j]["pos"][0]):
+            s0, v0 = val[j]
+            if need.get(s0) == v0:
+                for s, v in clock[j].items():
+                    if s != s0 and need.get(s, v + 1) <= v:
+                        del need[s]
+        for s in sorted(need):
+            queue[q].wait_ge(T.sem[s], need[s])
+        for j in hard:
+            for s, v in clock[j].items():
+                kn[s] = max(kn.get(s, 0), v)
+        ins = op["fn"](ctx)
+        total[name] = total.get(name, 0) + inc
+        val[i] = (name, total[name])
+        clock[i] = dict(kn)
+        clock[i][name] = total[name]
+        if not op.get("own"):
+            ins.then_inc(T.sem[name], inc)
+    for s in sorted(total):
+        if known["G"].get(s, 0) < total[s]:
+            g.wait_ge(T.sem[s], total[s])

@@ -4,12 +4,13 @@ ALU = AluOpType
 ACT = ActivationFunctionType
 ROUNDS, H, A0, NV, REC = 4, 128, 2048, 4096, 3584
 CHUNKS = ((0, 64), (64, 64))
-SCALAR_LANES = (64, 64)
-REP = "GGGGSSSSSSSSVVVV"
-REC_S = (0.5, 0.5)
-Z_S = ((1, 1),)
-MB_S = (1, 1)
-EQ_S = (0, 0)
+SCALAR_LANES = (128, 64)
+REP = "GGGSSSSSSVVVVVVV"
+REP0 = "SSSSSSSSVVVVVVVV"
+REC_S = (0.75, 0.5)
+Z_S = ((1, 0), (1, 1))
+EQ_S = (1, 0)
+C1STEP = 32
 
 F32, BF, I32, U16, F16 = "float32", "bfloat16", "int32", "uint16", "float16"
 LOGICAL = {}
@@ -22,9 +23,9 @@ def declare(dtype, **bufs):
 
 declare(BF, X=4112, Z=3072, pin=256, ones=2048, blk=128, gsp=144, gmin=144, gz=144, ghalf=144, g0b=144, idb=128, nidb=128, nid100=128,
         prmb=512, bcb=2048, wh=128, wl=128, rmask=1024, p=256, prep=4096)
-declare(F32, R=3072, whf=1, wlf=1, kf=1, cnt=1, bar=1, seg=128, ef=256, uf=128, pm=256, dd=256, yv=256, junk=128)
+declare(F32, R=3072, whf=1, wlf=1, kf=1, cnt=1, bar=1, seg=128, ef=256, dd=256, yv=256, junk=128)
 declare(I32, rti=2048, exi=256, wti=1, kmi=1, whi=1, wli=1, cnti=1, par=1, ui=128, u=128, uu=128, ku=128, su=128, hs=128, hh=128, pi=256)
-declare(F16, g0=144, nidh=128, idh=128, prm=512, bc=2048, ch=128, k2048=64)
+declare(F16, g0=144, nidh=128, idh=128, prm=512, bc=2048, ch=128, uh=128, k2048=64)
 declare(U16, cq=128)
 for _t in range(ROUNDS):
     declare(BF, **{"pn%d" % _t: 256, "Q%d" % _t: 128, "QL%d" % _t: 128})
@@ -52,7 +53,7 @@ for _n, (_w, _s, _d) in LOGICAL.items():
 for _b in range(8):
     LOGICAL["B%d" % _b] = SCRATCH["B%d" % _b] = ("psum", [128, 512], F32)
     PLACE["B%d" % _b] = ("B%d" % _b, 0)
-LOADS = ("p0", "wt", "km", "zp", "ax", "rt", "ex")
+LOADS = ("p0", "wt", "km", "zp", "rt", "ax", "ex")
 KINDS = ("p", "F", "L", "Q")
 SEMAPHORES = (["v", "s", "t", "gp", "out"] + ["ld_" + n for n in LOADS]
               + ["l%s%d" % (k, t) for k in KINDS for t in range(ROUNDS)] + ["a%s%d" % (k, t) for k in KINDS for t in range(ROUNDS)])
@@ -183,7 +184,7 @@ def build():
         return A(tab, 15 - x, 143 - x)
 
     load(A("pin"), "p0"); load(A("wti"), "wt"); load(A("kmi"), "km")
-    load(A("Z", 0, A0), "zp"); load(A("X", 0, NV), "ax"); load(A("rti"), "rt"); load(A("exi"), "ex")
+    load(A("Z", 0, A0), "zp"); load(A("rti"), "rt"); load(A("X", 0, NV), "ax"); load(A("exi"), "ex")
     fill(A("ones", 0, 128), 1.0)
     aff(A("blk"), A("ones", 0, 128), [[-16, 8], [0, 16]], ALU.is_ge, 0, 1)
     aff(A("blk"), A("blk"), [[16, 8], [0, 16]], ALU.is_ge, 15, -1)
@@ -257,14 +258,15 @@ def build():
         ts(A("hh"), A("hs"), 4095, ALU.bitwise_and)
         ts(A("cq"), A("hh"), (8 + t) / 16.0, ALU.mult, -15.0 / 32, ALU.add)
         for k in range(16):
-            if REP[k] == "S":
+            rep = (REP if t else REP0)[k]
+            if rep == "S":
                 act(A("prep", k, 4096, 16), A("p"))
-            elif REP[k] == "G":
+            elif rep == "G":
                 aff(A("prep", k, 4096, 16), A("p"), [[0, 256]], ALU.is_ge, 0, 0)
             else:
                 cp(A("prep", k, 4096, 16), A("p"))
         ts(A("ch"), A("cq"), 2048.0, ALU.subtract)
-        cp(A("uf"), A("u"))
+        ts(A("uh"), A("u"), 2048.0, ALU.subtract)
         for c, (j0, P) in enumerate(CHUNKS):
             for par, d in ((0, "de_%d" % c), (1, "do_%d" % c)):
                 b = 16 * (2 * j0 + par * P)
@@ -275,7 +277,7 @@ def build():
             j0, P = CHUNKS[c]
             b = 16 * (2 * j0 + par * P)
             for i, k in enumerate(range(0, 16 * P, 512)):
-                sb = ("B7", "B6")[i % 2]
+                sb = ("B7", "B%d" % (1 + c % 2))[i % 2]
                 mm([(A(sb), A("idb"), A("zg_%d" % c, k, k + 512), True, False), (A(sb), A("nidb"), A("prep", b + k, b + k + 512), False, True)])
                 act(A("%s_%d" % (("de", "do")[par], c), k, k + 512), A(sb), ACT.Abs)
         for c, (j0, P) in enumerate(CHUNKS):
@@ -299,9 +301,8 @@ def build():
             ts(A("au" + cs), A("B0", q0, q0 + L // 16), 2048.0, ALU.add)
             cp(A("eu" + cs), Ind(A("R", 0, n), A("au" + cs)))
             act(A("e" + cs), Ind(A("R", 0, n), A("au" + cs)))
-            for par in range(2):
-                act(A(tb, par * P, par * P + P), A("uf", j0, j0 + P))
-            act(A(tb, 128, 128 + L), A("e" + cs), bias=2464.0 * t - 131072.0, scale=32.0)
+            mm([(A(tb, par * P, par * P + P), A("idh"), A("uh", j0, j0 + P), True, True) for par in range(2)])
+            act(A(tb, 128, 128 + L), A("e" + cs), bias=2464.0 * t - 131072.0, scale=2080.0)
             act(A(tb, 256, 256 + L), A("e" + cs))
             tt(A("t1" + cs), A("e" + cs), A(tb, 0, L), ALU.mult)
             tt(A("nn" + cs), A("t1" + cs), A(tb, 128, 128 + L), ALU.add)
@@ -310,9 +311,9 @@ def build():
         for c, (j0, P) in enumerate(CHUNKS):
             L, bk, tb, cs = 2 * P, "B%d" % (1 + c % 2), "B%d" % (3 + c % 2), "_%d" % c
             b = 32 * j0
-            for h in range(2):
-                tt(A("c1" + cs, 16 * P * h, 16 * P * h + 16 * P), Ind(A("X", 0, NV), A("eu" + cs, h * P, h * P + P)),
-                   A("prep", b + 16 * P * h, b + 16 * P * h + 16 * P), ALU.is_ge)
+            for l0 in range(0, L, C1STEP):
+                tt(A("c1" + cs, 16 * l0, 16 * (l0 + C1STEP)), Ind(A("X", 0, NV), A("eu" + cs, l0, l0 + C1STEP)),
+                   A("prep", b + 16 * l0, b + 16 * (l0 + C1STEP)), ALU.is_ge)
             act(A("em" + cs), A("e" + cs), bias=-2048.0)
             tt(A(tb, 384, 384 + L), A("ef", 2 * j0, 2 * j0 + L), A(tb, 256, 256 + L), ALU.subtract)
             tt(A(tb, 0, L), A("e2" + cs), A(tb, 256, 256 + L), ALU.subtract)
@@ -332,11 +333,8 @@ def build():
             ns = SCALAR_LANES[c]
             for h in range(2):
                 mm([(A(bk, 128 + h * P, 128 + h * P + P), route("gsp", k), A("c1" + cs, 16 * P * h + k, 16 * P * h + 16 * P, 16), k == 0, k == 15) for k in range(16)])
-            if MB_S[c]:
-                act(A("sg" + cs), A(bk, 128, 128 + L), ACT.Sign, bias=A("bar"), scale=-1.0)
-                act(A("mb" + cs), A("sg" + cs), ACT.Relu)
-            else:
-                ts(A("mb" + cs), A(bk, 128, 128 + L), A("bar"), ALU.is_lt)
+            act(A("sg" + cs), A(bk, 128, 128 + L), ACT.Sign, bias=A("bar"), scale=-1.0)
+            act(A("mb" + cs), A("sg" + cs), ACT.Relu)
             act(A("r1" + cs), A(bk, 128, 128 + L), ACT.Relu, bias=-800.0, scale=100.0)
             if ns > 0:
                 act(A("g1c" + cs, 0, ns), A(bk, 128, 128 + ns), bias=-8.0)
@@ -344,11 +342,11 @@ def build():
                 act(A("g1c" + cs, ns, L), A(bk, 128 + ns, 128 + L))
             tt(A(tb, 128, 128 + L), A("mb" + cs), A(tb, 384, 384 + L), ALU.mult)
             tt(A("base" + cs), A(tb, 128, 128 + L), A("em" + cs), ALU.add)
-            for lo, hi, tab in [(0, ns, "ghalf")] * (ns > 0) + [(l0, min(l0 + 64, L), "gsp") for l0 in range(ns, L, 64)]:
+            for lo, hi, tab in [(l0, min(l0 + 64, L), "gsp") for l0 in range(ns, L, 64)] + [(0, ns, "ghalf")] * (ns > 0):
                 o = A(bk, 256 + lo, 256 + hi)
-                mm([(o, A("nid100"), A("mb" + cs, lo, hi), True, False), (o, A("nidb"), A("r1" + cs, lo, hi), False, False),
-                    (o, A("nidb"), A("g1c" + cs, lo, hi), False, False)]
-                   + [(o, route(tab, k), A("c2" + cs, 16 * lo + k, 16 * hi, 16), False, k == 15) for k in range(16)])
+                mm([(o, route(tab, k), A("c2" + cs, 16 * lo + k, 16 * hi, 16), k == 0, False) for k in range(16)])
+                mm([(o, A("nid100"), A("mb" + cs, lo, hi), False, False), (o, A("nidb"), A("r1" + cs, lo, hi), False, False),
+                    (o, A("nidb"), A("g1c" + cs, lo, hi), False, True)])
             ts(A("ma" + cs), A(bk, 256, 256 + L), 0.0, ALU.is_ge)
             tt(A(tb, 256, 256 + L), A("ma" + cs), A(tb, 0, L), ALU.mult)
             tt(A("f" + cs), A(tb, 256, 256 + L), A("base" + cs), ALU.add)
@@ -368,10 +366,13 @@ def build():
                     act(x, y, ACT.Relu, bias=1.0, scale=-1.0)
                 else:
                     ts(x, A(eb, 0, 8 * P), 0.0, ALU.is_equal)
-            for par in range(2):
-                mm([(A(bk, 384 + par * P, 384 + par * P + P), route("gsp", k) if par else A("idb"), A("eq" + cs, k * P, k * P + P), k == 0, k == 15) for k in range(16)])
+            for h in range(2):
+                for par in range(2):
+                    mm([(A(("B7" if par else bk), 384, 384 + P), route("gsp", k) if par else A("idb"), A("eq" + cs, k * P, k * P + P), k == 0, k == 15)
+                        for k in range(8 * h, 8 * h + 8)])
             act(A(tb, 384, 384 + P), A(bk, 384, 384 + P), bias=2048.0, scale=-8192.0)
-            act(A("cm" + cs), A(bk, 384, 384 + L), ACT.Sign)
+            act(A("cm" + cs, P, L), A("B7", 384, 384 + P), ACT.Sign)
+            act(A("cm" + cs, 0, P), A(bk, 384, 384 + P), ACT.Sign)
             tt(A("rt1" + cs), A(tb, 384, 384 + P), A("f" + cs, 0, P), ALU.max)
             ts(A("ro" + cs), A("rt1" + cs), 2048.0, ALU.add)
             ps = int(P * REC_S[c]) // 16 * 16
@@ -400,19 +401,17 @@ def build():
             ts(A("par"), A("cnti"), 1, ALU.bitwise_and)
             ts(A("bar"), A("par"), 3.5, ALU.add)
         store("yr", 256 * t, 256 * t + 256, A("R", n, n + 256))
-        for c, (j0, P) in enumerate(CHUNKS):
-            for par in range(2):
-                act(A("pm", 2 * j0 + par * P, 2 * j0 + par * P + P), A("Z", n + 2 * j0 + par, n + 2 * j0 + 2 * P, 2), bias=255.0)
         cp(A("X", REC + H * t, REC + H * t + H), A("QL%d" % t))
-        tt(A("dd"), Ind(A("X", 0, NV), A("LL%d" % t)), A("pm"), ALU.subtract)
-        ts(A("pi"), A("dd"), -0.5, ALU.mult, -0.25, ALU.add)
-        if t < ROUNDS - 1:
-            cp(A("p"), A("pi"))
-        else:
+        for par in range(2):
             for c, (j0, P) in enumerate(CHUNKS):
-                for par in range(2):
-                    cp(A("yv", 2 * j0 + par, 2 * j0 + 2 * P, 2), A("pi", 2 * j0 + par * P, 2 * j0 + par * P + P))
-            store("yp", 0, 256, A("yv"))
+                lo, hi = 2 * j0 + par * P, 2 * j0 + par * P + P
+                tt(A("dd", lo, hi), Ind(A("X", 0, NV), A("LL%d" % t, lo // 16, hi // 16)), A("Z", n + 2 * j0 + par, n + 2 * j0 + 2 * P, 2), ALU.subtract)
+                ts(A("pi", lo, hi), A("dd", lo, hi), -0.5, ALU.mult, 127.25, ALU.add)
+                if t < ROUNDS - 1:
+                    cp(A("p", lo, hi), A("pi", lo, hi))
+                else:
+                    cp(A("yv", 2 * j0 + par, 2 * j0 + 2 * P, 2), A("pi", lo, hi))
+    store("yp", 0, 256, A("yv"))
     return ops
 
 
@@ -429,14 +428,11 @@ def dependencies(ops):
         deps = {}
         acc = [(a, False) for a in op["ins"]] + [(a, True) for a in op["outs"]]
         for a, wr in acc:
-            bank = a[0] in PSUM
             for j, b, bw in hist.setdefault(a[0], []):
                 same = ops[j]["q"] == op["q"]
                 if (wr or bw) and overlap(a, b):
-                    deps[j] = deps.get(j, False) or not same or (bw and not wr)
-                elif bank and not same:
-                    deps[j] = True
-                elif bank and op["q"] == "P":
+                    deps[j] = deps.get(j, False) or not same or op["q"] != "P"
+                elif same and a[0] in PSUM and op["q"] == "P":
                     deps[j] = deps.get(j, False)
         for a, wr in acc:
             h = hist[a[0]]
@@ -446,9 +442,13 @@ def dependencies(ops):
                 h[:] = [e for e in h if not (e[0] != i and e[1][1] >= a[1] and e[1][2] <= a[2])]
             h.append((i, a, wr))
         op["deps"] = deps
+        op["banks"] = {a[0] for a, _ in acc if a[0] in PSUM}
 
 
-def schedule(ops, slack=0.0, wake=0.12):
+LOOK, BIG = 0.2, 0.45
+
+
+def schedule(ops, wake=0.25):
     n = len(ops)
     succ = [[] for _ in range(n)]
     npred = [0] * n
@@ -461,7 +461,7 @@ def schedule(ops, slack=0.0, wake=0.12):
     for i in range(n - 1, -1, -1):
         b = max([prio[k] + (0.0 if ops[k]["q"] == ops[i]["q"] else wake) for k in succ[i]] + [0.0])
         prio[i] = b + ops[i]["cost"] + ops[i].get("lat", 0.0)
-    free, count, done = {}, {}, [0.0] * n
+    free, count, done, last = {}, {}, [0.0] * n, {}
     ready = {i for i in range(n) if npred[i] == 0}
     while ready:
         best = {}
@@ -470,15 +470,27 @@ def schedule(ops, slack=0.0, wake=0.12):
             s = free.get(q, 0.0) if q != "R" else 0.0
             for j in ops[i]["preds"]:
                 s = max(s, done[j] + (wake if ops[j]["q"] != q else 0.02))
+            for b in ops[i]["banks"]:
+                for q2, j in last.get(b, {}).items():
+                    if q2 != q:
+                        s = max(s, done[j] + wake)
             best.setdefault(q, []).append((s, i))
         pick = None
         for q, lst in sorted(best.items()):
             m = min(s for s, _ in lst)
-            s, i = max(((s, i) for s, i in lst if s <= m + slack), key=lambda e: (prio[e[1]], -e[1]))
+            s, i = max(((s, i) for s, i in lst if s <= m), key=lambda e: (prio[e[1]], -e[1]))
+            if ops[i]["cost"] > BIG:
+                s, i = max(((s, i) for s, i in lst if s <= m + LOOK), key=lambda e: (prio[e[1]], -e[1]))
             if pick is None or (s, -prio[i]) < pick[:2]:
                 pick = (s, -prio[i], i, q)
         s, _, i, q = pick
         ready.remove(i)
+        for b in ops[i]["banks"]:
+            users = last.setdefault(b, {})
+            for q2, j in users.items():
+                if q2 != q:
+                    ops[i]["deps"][j] = True
+            users[q] = i
         free[q] = s + ops[i]["cost"]
         done[i] = s + ops[i]["cost"] + ops[i].get("lat", 0.0)
         count[q] = count.get(q, 0) + 1

from concourse.mybir import AluOpType, ActivationFunctionType

ALU = AluOpType
ACT = ActivationFunctionType
ROUNDS, H, A0, NV, REC = 4, 128, 2048, 4096, 3584
CHUNKS = ((0, 64), (64, 64))
SCALAR_LANES = (128, 64)
REP = "GGGSSSSSSVVVVVVV"
REP0 = "SSSSSSSSVVVVVVVV"
REC_S = (0.75, 0.5)
Z_S = ((1, 0), (1, 1))
EQ_S = (1, 0)
C1STEP = 32

F32, BF, I32, U16, F16 = "float32", "bfloat16", "int32", "uint16", "float16"
LOGICAL = {}


def declare(dtype, **bufs):
    for n, w in bufs.items():
        LOGICAL[n] = ("sbuf", [128, w], dtype)


declare(BF, X=4112, Z=3072, pin=256, ones=2048, blk=128, gsp=144, gmin=144, gz=144, ghalf=144, g0b=144, idb=128, nidb=128, nid100=128,
        prmb=512, bcb=2048, wh=128, wl=128, rmask=1024, p=256, prep=4096)
declare(F32, R=3072, whf=1, wlf=1, kf=1, cnt=1, bar=1, seg=128, ef=256, dd=256, yv=256, junk=128)
declare(I32, rti=2048, exi=256, wti=1, kmi=1, whi=1, wli=1, cnti=1, par=1, ui=128, u=128, uu=128, ku=128, su=128, hs=128, hh=128, pi=256)
declare(F16, g0=144, nidh=128, idh=128, prm=512, bc=2048, ch=128, uh=128, k2048=64)
declare(U16, cq=128)
for _t in range(ROUNDS):
    declare(BF, **{"pn%d" % _t: 256, "Q%d" % _t: 128, "QL%d" % _t: 128})
    declare(F32, **{"F%d" % _t: 256, "nr%d" % _t: 256})
    declare(U16, **{"LT%d" % _t: 16, "LL%d" % _t: 16})
for _c, (_j, _p) in enumerate(CHUNKS):
    _l = 2 * _p
    for _d, _names in ((BF, (("de", 16 * _p), ("do", 16 * _p), ("zg", 16 * _p), ("ez", 16 * _p), ("c1", 16 * _l), ("c2", 16 * _l), ("xg", 16 * _l),
                             ("mb", _l), ("r1", _l), ("g1c", _l), ("eq", 16 * _p), ("cm", _l), ("xr", 16 * _p), ("qs", 16 * _p))),
                       (F32, (("tr", _l), ("sg", _l), ("e", _l), ("em", _l), ("t1", _l), ("base", _l), ("ma", _l), ("rt1", _p))),
                       (I32, (("mk", _l), ("ai", _l // 16), ("nn", _l), ("e2", _l))),
                       (F16, (("ah", _l // 16), ("f", _l), ("fh", _l))),
                       (U16, (("au", _l // 16), ("eu", _l), ("e2u", _l), ("ro", _p)))):
        declare(_d, **{"%s_%d" % (n, _c): w for n, w in _names})
OWN = {"X", "Z", "R", "rti", "exi", "pin", "wti", "kmi"} | {"%s%d" % (n, t) for n in ("pn", "F", "Q", "QL", "LT", "LL") for t in range(ROUNDS)}
SCRATCH, PLACE = {}, {}
for _n, (_w, _s, _d) in LOGICAL.items():
    if _n in OWN:
        SCRATCH[_n], PLACE[_n] = (_w, _s, _d), (_n, 0)
    else:
        _k = "pool_" + _d
        _o = SCRATCH.get(_k, (0, [128, 0]))[1][1]
        PLACE[_n] = (_k, _o)
        SCRATCH[_k] = ("sbuf", [128, _o + (_s[1] + 31) // 32 * 32], _d)
for _b in range(8):
    LOGICAL["B%d" % _b] = SCRATCH["B%d" % _b] = ("psum", [128, 512], F32)
    PLACE["B%d" % _b] = ("B%d" % _b, 0)
LOADS = ("p0", "wt", "km", "zp", "rt", "ax", "ex")
KINDS = ("p", "F", "L", "Q")
SEMAPHORES = (["v", "s", "t", "gp", "out"] + ["ld_" + n for n in LOADS]
              + ["l%s%d" % (k, t) for k in KINDS for t in range(ROUNDS)] + ["a%s%d" % (k, t) for k in KINDS for t in range(ROUNDS)])
WIDTH = {n: s[1][1] for n, s in LOGICAL.items()}
PSUM = {n for n, s in LOGICAL.items() if s[0] == "psum"}
TWO = {n for n, s in LOGICAL.items() if s[2] in (BF, F16, U16)}
CYC, GATHER = 1.0e-3, 1.55


def A(name, lo=0, hi=None, st=1):
    return (name, lo, WIDTH[name] if hi is None else hi, st)


def Ind(win, off):
    return ("@", win, off)


def size(a):
    return 16 * size(a[2]) if a[0] == "@" else (a[2] - a[1] + a[3] - 1) // a[3]


def ap(T, a):
    if a[0] == "@":
        return ap(T, a[1]).indirect(ap(T, a[2]))
    name, o = PLACE[a[0]]
    if a[3] == 1:
        return T[name][:, o + a[1]:o + a[2]]
    return T[name][:, o + a[1]:o + a[2]:a[3]]


def flat(aps):
    out = []
    for a in aps:
        if isinstance(a, tuple):
            out += [a[1], a[2]] if a[0] == "@" else [a]
    return out


def build():
    ops = []

    def add(q, cost, outs, ins, fn, **kw):
        op = dict(q=q, cost=cost, outs=flat(outs), ins=flat(ins), fn=fn, **kw)
        ops.append(op)
        return op

    def vcost(aps, mode):
        n = size(aps[0])
        if any(a[0] == "@" for a in aps):
            return 0.06 + n * GATHER * CYC
        per = 1.0
        if mode == "tt":
            per = 1.0 if any(a[0] in PSUM for a in aps[1:]) else 2.0
        elif all(a[0] in TWO for a in aps):
            per = 0.5
        return 0.06 + max(64, n * per) * CYC

    def tt(out, a, b, op):
        add("V", vcost((out, a, b), "tt"), [out], [a, b], lambda c: c["V"].tensor_tensor(ap(c["T"], out), ap(c["T"], a), ap(c["T"], b), op))

    def ts(out, a, s1, op0, s2=None, op1=None):
        def fn(c):
            x1 = ap(c["T"], s1) if isinstance(s1, tuple) else s1
            if op1 is None:
                return c["V"].tensor_scalar(ap(c["T"], out), ap(c["T"], a), x1, None, op0)
            return c["V"].tensor_scalar(ap(c["T"], out), ap(c["T"], a), x1, s2, op0, op1)
        add("V", vcost((out, a), "ts"), [out], [a, s1], fn)

    def cp(out, a):
        add("V", vcost((out, a), "ts"), [out], [a], lambda c: c["V"].tensor_copy(ap(c["T"], out), ap(c["T"], a)))

    def fill(out, val):
        add("V", 0.06 + size(out) * CYC, [out], [], lambda c: c["V"].memset(ap(c["T"], out), val))

    def scan(out, d0, d1, op0, op1):
        add("V", vcost((out, d0, d1), "ts"), [out], [d0, d1],
            lambda c: c["V"].tensor_tensor_scan(ap(c["T"], out), ap(c["T"], d0), ap(c["T"], d1), 0.0, op0, op1))

    def vtr(out, a):
        add("V", vcost((out, a), "ts"), [out], [a], lambda c: c["V"].transpose(ap(c["T"], out), ap(c["T"], a)))

    def act(out, a, func=None, bias=0.0, scale=1.0, accum=None):
        func = ACT.Identity if func is None else func
        n = size(out)

        def fn(c):
            x = ap(c["T"], accum) if accum is not None else None
            b = ap(c["T"], bias) if isinstance(bias, tuple) else bias
            return c["S"].activation(ap(c["T"], out), ap(c["T"], a), func, bias=b, scale=scale, accum_out=x)
        add("S", 0.08 + n * CYC * (GATHER if a[0] == "@" else 1.0), [out] + ([accum] if accum is not None else []), [a, bias], fn)

    def mm(items):
        def fn(c):
            m = None
            for o, l, r, s, e in items:
                m = c["P"].matmul(ap(c["T"], o), ap(c["T"], l), ap(c["T"], r), s, e)
            return m
        outs, ins = [], []
        for o, l, r, s, e in items:
            for x, d in ((o, outs), (l, ins), (r, ins)):
                if x not in d:
                    d.append(x)
        add("P", sum(max(64, size(i[2])) for i in items) * 0.5e-3 + 0.02, outs, ins, fn)

    def aff(out, a, pattern, cmp, base, cm):
        add("G", 0.2 + 2 * size(out) * CYC, [out], [a], lambda c: c["g"].affine_select(ap(c["T"], out), ap(c["T"], a), pattern, cmp, 0.0, base, cm), sem="gp")

    def iota(out, pattern, base):
        add("G", 0.15 + 2 * size(out) * CYC, [out], [], lambda c: c["g"].iota(ap(c["T"], out), pattern, base, 0, allow_small_or_imprecise_dtypes=True), sem="gp")

    def load(out, name):
        add("Y", 0.15, [out], [], lambda c: c["g"].sync.dma_start(ap(c["T"], out), c["T"][name][:]), sem="ld_" + name, inc=16, lat=2.0 + size(out) / 2000.0)

    def store(name, lo, hi, a):
        add("Y", 0.15, [], [a], lambda c: c["g"].sync.dma_start(c["T"][name][:, lo:hi], ap(c["T"], a)), sem="out", inc=16, lat=2.0)

    def send(kind, t, dst, src):
        def fn(c):
            to = c["T"].cores[(c["rank"] + 1 + t % 3) % len(c["T"].cores)]
            topo = c["topo"]
            rid, pid, _ = topo.addr(to)
            c["g"].remote_dma(ap(c["T"], dst), ap(c["T"], src), c["T"].sem["a%s%d" % (kind, t)], c["T"].sem["l%s%d" % (kind, t)],
                              pid, rid, topo.mask(c["core"], to))
        s = add("G", 0.2, [], [src], fn, sem="l%s%d" % (kind, t), inc=16, own=True, lat=2.0)
        add("R", 0.0, [dst], [], None, sem="a%s%d" % (kind, t), inc=16, after=s, lat=2.2)

    def route(tab, x):
        return A(tab, 15 - x, 143 - x)

    load(A("pin"), "p0"); load(A("wti"), "wt"); load(A("kmi"), "km")
    load(A("Z", 0, A0), "zp"); load(A("rti"), "rt"); load(A("X", 0, NV), "ax"); load(A("exi"), "ex")
    fill(A("ones", 0, 128), 1.0)
    aff(A("blk"), A("ones", 0, 128), [[-16, 8], [0, 16]], ALU.is_ge, 0, 1)
    aff(A("blk"), A("blk"), [[16, 8], [0, 16]], ALU.is_ge, 15, -1)
    for c, (j0, P) in enumerate(CHUNKS):
        for par in range(2):
            cp(A("p", 2 * j0 + par * P, 2 * j0 + par * P + P), A("pin", 2 * j0 + par, 2 * j0 + 2 * P, 2))
    ts(A("whi"), A("wti"), 6, ALU.logical_shift_right)
    ts(A("wli"), A("wti"), 63, ALU.bitwise_and)
    ts(A("whf"), A("whi"), 64.0, ALU.mult)
    cp(A("wlf"), A("wli"))
    ts(A("wh"), A("blk"), A("whf"), ALU.mult)
    ts(A("wl"), A("blk"), A("wlf"), ALU.mult)
    ts(A("kf"), A("kmi"), 4096.0, ALU.subtract)
    send("p", 0, A("Z", A0, A0 + 256), A("pin"))
    fill(A("gsp"), 0.0)
    aff(A("gsp", 15, 143, 16), A("ones", 0, 8), [[-16, 8]], ALU.is_ge, 0, 1)
    aff(A("gsp", 15, 143, 16), A("gsp", 15, 143, 16), [[16, 8]], ALU.is_ge, 15, -1)
    act(A("gmin"), A("gsp"), scale=-8192.0)
    act(A("gz"), A("gsp"), scale=4096.0)
    act(A("ghalf"), A("gsp"), scale=0.5)
    fill(A("seg"), 0.0)
    fill(A("seg", 0, 128, 16), 1e9)
    for qh in range(2):
        for gp in range(2):
            k = 128 * (2 * qh + gp)
            aff(A("prmb", k, k + 128), A("ones", 0, 128), [[-32, 4], [-1000, 2], [-1, 16]], ALU.is_equal, 1000 * gp - 16 * qh, 1)
    cp(A("prm"), A("prmb"))
    aff(A("idb"), A("ones", 0, 128), [[-1, 128]], ALU.is_equal, 0, 1)
    act(A("nidb"), A("idb"), scale=-1.0)
    act(A("nid100"), A("idb"), scale=-100.0)
    ts(A("nidh"), A("idb"), -1.0, ALU.mult)
    cp(A("idh"), A("idb"))
    ts(A("k2048"), A("ones", 0, 64), 2048.0, ALU.mult)
    fill(A("bar"), 3.5)
    fill(A("ones", 128, 2048), 1.0)
    aff(A("bcb"), A("ones"), [[-1, 16], [-16, 8], [0, 16]], ALU.is_equal, 0, 1)
    fill(A("X", NV, NV + 16), 0.0)
    fill(A("rmask"), 1.0)
    fill(A("rmask", 0, 1024, 16), 0.0)
    fill(A("g0b"), 0.0)
    aff(A("g0b", 15, 143, 16), A("ones", 0, 8), [[-16, 8]], ALU.is_equal, 0, 1)
    for k in range(0, 2048, 512):
        cp(A("bc", k, k + 512), A("bcb", k, k + 512))
    cp(A("g0"), A("g0b"))
    for t in range(ROUNDS):
        for c, (j0, P) in enumerate(CHUNKS):
            iota(A("nr%d" % t, 2 * j0, 2 * j0 + 2 * P), [[0, 2], [1, P]], REC - 2048 + H * t + j0)
    for k in range(0, A0, 512):
        cp(A("R", k, k + 512), A("rti", k, k + 512))
    for c, (j0, P) in enumerate(CHUNKS):
        for par in range(2):
            cp(A("ef", 2 * j0 + par * P, 2 * j0 + par * P + P), A("exi", 2 * j0 + par, 2 * j0 + 2 * P, 2))

    for t in range(ROUNDS):
        n = A0 + 256 * t
        NC = len(CHUNKS)
        if t > 0:
            for c, (j0, P) in enumerate(CHUNKS):
                for par in range(2):
                    aff(A("pn%d" % t, 2 * j0 + par, 2 * j0 + 2 * P, 2), A("p", 2 * j0 + par * P, 2 * j0 + par * P + P), [[0, P]], ALU.is_ge, 0, 0)
            send("p", t, A("Z", n, n + 256), A("pn%d" % t))
        for c, (j0, P) in enumerate(CHUNKS):
            mm([(A("B0", j0, j0 + P), A("wh"), A("p", 2 * j0, 2 * j0 + P), True, False),
                (A("B0", j0, j0 + P), A("wl"), A("p", 2 * j0, 2 * j0 + P), False, True)])
        cp(A("ui"), A("B0", 0, 128))
        ts(A("u"), A("ui"), 4095, ALU.bitwise_and)
        tt(A("uu"), A("u"), A("u"), ALU.mult)
        ts(A("ku"), A("u"), A("kf"), ALU.mult)
        ts(A("su"), A("uu"), 5, ALU.logical_shift_right)
        tt(A("hs"), A("su"), A("ku"), ALU.add)
        ts(A("hh"), A("hs"), 4095, ALU.bitwise_and)
        ts(A("cq"), A("hh"), (8 + t) / 16.0, ALU.mult, -15.0 / 32, ALU.add)
        for k in range(16):
            rep = (REP if t else REP0)[k]
            if rep == "S":
                act(A("prep", k, 4096, 16), A("p"))
            elif rep == "G":
                aff(A("prep", k, 4096, 16), A("p"), [[0, 256]], ALU.is_ge, 0, 0)
            else:
                cp(A("prep", k, 4096, 16), A("p"))
        ts(A("ch"), A("cq"), 2048.0, ALU.subtract)
        ts(A("uh"), A("u"), 2048.0, ALU.subtract)
        for c, (j0, P) in enumerate(CHUNKS):
            for par, d in ((0, "de_%d" % c), (1, "do_%d" % c)):
                b = 16 * (2 * j0 + par * P)
                if (c, par) not in Z_S:
                    tt(A(d), Ind(A("Z", 0, n), A("cq", j0, j0 + P)), A("prep", b, b + 16 * P), ALU.min)
            act(A("zg_%d" % c), Ind(A("Z", 0, n), A("cq", j0, j0 + P)))
        for c, par in Z_S:
            j0, P = CHUNKS[c]
            b = 16 * (2 * j0 + par * P)
            for i, k in enumerate(range(0, 16 * P, 512)):
                sb = ("B7", "B%d" % (1 + c % 2))[i % 2]
                mm([(A(sb), A("idb"), A("zg_%d" % c, k, k + 512), True, False), (A(sb), A("nidb"), A("prep", b + k, b + k + 512), False, True)])
                act(A("%s_%d" % (("de", "do")[par], c), k, k + 512), A(sb), ACT.Abs)
        for c, (j0, P) in enumerate(CHUNKS):
            L, bk, tb, cs = 2 * P, "B%d" % (1 + c % 2), "B%d" % (3 + c % 2), "_%d" % c
            for par, d in ((0, "de"), (1, "do")):
                o = A(bk, par * P, par * P + P)
                mm([(o, A("idh"), A("k2048", 0, P), True, False), (o, A("idh"), A("ch", j0, j0 + P), False, False)]
                   + [(o, route("gz", m), A("zg" + cs, m, 16 * P, 16), False, False) for m in range(16) if (c, par) not in Z_S])
                mm([(o, route("gz" if (c, par) in Z_S else "gmin", m), A(d + cs, m, 16 * P, 16), False, m == 15) for m in range(16)])
            vtr(A("tr" + cs), A(bk, 0, L))
            scan(A("mk" + cs), A("seg", 0, L), A("tr" + cs), ALU.add, ALU.min)
            ts(A("ai" + cs), A("mk" + cs, 15, L, 16), 4095, ALU.bitwise_and)
            ts(A("ah" + cs), A("ai" + cs), 2048.0, ALU.subtract)
            q0 = 128 + 2 * j0 // 16
            items = []
            for qh in range(2):
                for gp in range(2):
                    k = 128 * (2 * qh + gp)
                    items.append((A("B0", q0 + qh, q0 + L // 16, 2), A("prm", k, k + 128), A("ah" + cs, gp, L // 16, 2), gp == 0, gp == 1))
            mm(items)
            ts(A("au" + cs), A("B0", q0, q0 + L // 16), 2048.0, ALU.add)
            cp(A("eu" + cs), Ind(A("R", 0, n), A("au" + cs)))
            act(A("e" + cs), Ind(A("R", 0, n), A("au" + cs)))
            mm([(A(tb, par * P, par * P + P), A("idh"), A("uh", j0, j0 + P), True, True) for par in range(2)])
            act(A(tb, 128, 128 + L), A("e" + cs), bias=2464.0 * t - 131072.0, scale=2080.0)
            act(A(tb, 256, 256 + L), A("e" + cs))
            tt(A("t1" + cs), A("e" + cs), A(tb, 0, L), ALU.mult)
            tt(A("nn" + cs), A("t1" + cs), A(tb, 128, 128 + L), ALU.add)
            ts(A("e2" + cs), A("nn" + cs), 5, ALU.arith_shift_right, 4095, ALU.bitwise_and)
            cp(A("e2u" + cs), A("e2" + cs))
        for c, (j0, P) in enumerate(CHUNKS):
            L, bk, tb, cs = 2 * P, "B%d" % (1 + c % 2), "B%d" % (3 + c % 2), "_%d" % c
            b = 32 * j0
            for l0 in range(0, L, C1STEP):
                tt(A("c1" + cs, 16 * l0, 16 * (l0 + C1STEP)), Ind(A("X", 0, NV), A("eu" + cs, l0, l0 + C1STEP)),
                   A("prep", b + 16 * l0, b + 16 * (l0 + C1STEP)), ALU.is_ge)
            act(A("em" + cs), A("e" + cs), bias=-2048.0)
            tt(A(tb, 384, 384 + L), A("ef", 2 * j0, 2 * j0 + L), A(tb, 256, 256 + L), ALU.subtract)
            tt(A(tb, 0, L), A("e2" + cs), A(tb, 256, 256 + L), ALU.subtract)
            ns = SCALAR_LANES[c]
            for i, l0 in enumerate(range(0, ns, 32)):
                sb = ("B7", "B6" if c == 0 else "B0")[i % 2]
                x = A("xg" + cs, 16 * l0, 16 * (l0 + 32))
                act(x, Ind(A("X", 0, NV), A("e2u" + cs, l0, l0 + 32)))
                mm([(A(sb), A("idb"), x, True, False),
                    (A(sb), A("nidb"), A("prep", b + 16 * l0, b + 16 * (l0 + 32)), False, True)])
                act(A("c2" + cs, 16 * l0, 16 * (l0 + 32)), A(sb), ACT.Sign, bias=0.5)
            for l0 in range(ns, L, 64):
                hi = min(l0 + 64, L)
                tt(A("c2" + cs, 16 * l0, 16 * hi), Ind(A("X", 0, NV), A("e2u" + cs, l0, hi)), A("prep", b + 16 * l0, b + 16 * hi), ALU.is_ge)
        for c, (j0, P) in enumerate(CHUNKS):
            L, bk, tb, cs = 2 * P, "B%d" % (1 + c % 2), "B%d" % (3 + c % 2), "_%d" % c
            ns = SCALAR_LANES[c]
            for h in range(2):
                mm([(A(bk, 128 + h * P, 128 + h * P + P), route("gsp", k), A("c1" + cs, 16 * P * h + k, 16 * P * h + 16 * P, 16), k == 0, k == 15) for k in range(16)])
            act(A("sg" + cs), A(bk, 128, 128 + L), ACT.Sign, bias=A("bar"), scale=-1.0)
            act(A("mb" + cs), A("sg" + cs), ACT.Relu)
            act(A("r1" + cs), A(bk, 128, 128 + L), ACT.Relu, bias=-800.0, scale=100.0)
            if ns > 0:
                act(A("g1c" + cs, 0, ns), A(bk, 128, 128 + ns), bias=-8.0)
            if ns < L:
                act(A("g1c" + cs, ns, L), A(bk, 128 + ns, 128 + L))
            tt(A(tb, 128, 128 + L), A("mb" + cs), A(tb, 384, 384 + L), ALU.mult)
            tt(A("base" + cs), A(tb, 128, 128 + L), A("em" + cs), ALU.add)
            for lo, hi, tab in [(l0, min(l0 + 64, L), "gsp") for l0 in range(ns, L, 64)] + [(0, ns, "ghalf")] * (ns > 0):
                o = A(bk, 256 + lo, 256 + hi)
                mm([(o, route(tab, k), A("c2" + cs, 16 * lo + k, 16 * hi, 16), k == 0, False) for k in range(16)])
                mm([(o, A("nid100"), A("mb" + cs, lo, hi), False, False), (o, A("nidb"), A("r1" + cs, lo, hi), False, False),
                    (o, A("nidb"), A("g1c" + cs, lo, hi), False, True)])
            ts(A("ma" + cs), A(bk, 256, 256 + L), 0.0, ALU.is_ge)
            tt(A(tb, 256, 256 + L), A("ma" + cs), A(tb, 0, L), ALU.mult)
            tt(A("f" + cs), A(tb, 256, 256 + L), A("base" + cs), ALU.add)
            tt(A(tb, 0, L), A("nr%d" % t, 2 * j0, 2 * j0 + L), A("f" + cs), ALU.subtract)
            for h in range(2):
                eb = "B%d" % (5 + h)
                items = []
                for k in range(8):
                    o = A(eb, k * P, k * P + P)
                    items.append((o, A("nidh"), A("f" + cs, 0, P), True, False))
                    items.append((o, A("bc", 128 * (8 * h + k), 128 * (8 * h + k) + 128), A("f" + cs, P, L), False, True))
                mm(items)
                x = A("eq" + cs, 8 * P * h, 8 * P * h + 8 * P)
                if EQ_S[c]:
                    y = A("ez" + cs, 8 * P * h, 8 * P * h + 8 * P)
                    act(y, A(eb, 0, 8 * P), ACT.Abs)
                    act(x, y, ACT.Relu, bias=1.0, scale=-1.0)
                else:
                    ts(x, A(eb, 0, 8 * P), 0.0, ALU.is_equal)
            for h in range(2):
                for par in range(2):
                    mm([(A(("B7" if par else bk), 384, 384 + P), route("gsp", k) if par else A("idb"), A("eq" + cs, k * P, k * P + P), k == 0, k == 15)
                        for k in range(8 * h, 8 * h + 8)])
            act(A(tb, 384, 384 + P), A(bk, 384, 384 + P), bias=2048.0, scale=-8192.0)
            act(A("cm" + cs, P, L), A("B7", 384, 384 + P), ACT.Sign)
            act(A("cm" + cs, 0, P), A(bk, 384, 384 + P), ACT.Sign)
            tt(A("rt1" + cs), A(tb, 384, 384 + P), A("f" + cs, 0, P), ALU.max)
            ts(A("ro" + cs), A("rt1" + cs), 2048.0, ALU.add)
            ps = int(P * REC_S[c]) // 16 * 16
            if ps:
                act(A("xr" + cs, 0, 16 * ps), Ind(A("X"), A("ro" + cs, 0, ps)))
            if ps < P:
                cp(A("xr" + cs, 16 * ps, 16 * P), Ind(A("X"), A("ro" + cs, ps, P)))
            tt(A(tb, 128, 128 + L), A("cm" + cs), A(tb, 0, L), ALU.mult)
            tt(A("fh" + cs), A(tb, 128, 128 + L), A("f" + cs), ALU.add)
            for par in range(2):
                mm([(A("B0", 256 + 2 * j0 + par, 256 + 2 * j0 + L, 2), A("nidh"), A("fh" + cs, par * P, par * P + P), True, True)])
            act(A("F%d" % t, 2 * j0, 2 * j0 + L), A("B0", 256 + 2 * j0, 256 + 2 * j0 + L), bias=2048.0, scale=-1.0)
            q0 = 160 + 2 * j0 // 16
            mm([(A("B0", q0, q0 + L // 16), route("g0", x), A("fh" + cs, x, L, 16), x == 0, x == 15) for x in range(16)])
            ts(A("LT%d" % t, 2 * j0 // 16, 2 * j0 // 16 + L // 16), A("B0", q0, q0 + L // 16), 2048.0, ALU.add)
            scan(A("qs" + cs), A("rmask", 0, 16 * P), A("xr" + cs), ALU.mult, ALU.max)
            cp(A("Q%d" % t, j0, j0 + P), A("qs" + cs, 15, 16 * P, 16))
        send("F", t, A("R", n, n + 256), A("F%d" % t))
        send("L", t, A("LL%d" % t), A("LT%d" % t))
        send("Q", t, A("QL%d" % t), A("Q%d" % t))
        if t < ROUNDS - 1:
            mm([(A("B7", 0, 2 * P), A("ones", 0, 128), A("mb_%d" % c), c == 0, c == NC - 1) for c, (j0, P) in enumerate(CHUNKS)])
            P0 = CHUNKS[0][1]
            act(A("junk", 0, 2 * P0), A("B7", 0, 2 * P0), accum=A("cnt"))
            cp(A("cnti"), A("cnt"))
            ts(A("par"), A("cnti"), 1, ALU.bitwise_and)
            ts(A("bar"), A("par"), 3.5, ALU.add)
        store("yr", 256 * t, 256 * t + 256, A("R", n, n + 256))
        cp(A("X", REC + H * t, REC + H * t + H), A("QL%d" % t))
        for par in range(2):
            for c, (j0, P) in enumerate(CHUNKS):
                lo, hi = 2 * j0 + par * P, 2 * j0 + par * P + P
                tt(A("dd", lo, hi), Ind(A("X", 0, NV), A("LL%d" % t, lo // 16, hi // 16)), A("Z", n + 2 * j0 + par, n + 2 * j0 + 2 * P, 2), ALU.subtract)
                ts(A("pi", lo, hi), A("dd", lo, hi), -0.5, ALU.mult, 127.25, ALU.add)
                if t < ROUNDS - 1:
                    cp(A("p", lo, hi), A("pi", lo, hi))
                else:
                    cp(A("yv", 2 * j0 + par, 2 * j0 + 2 * P, 2), A("pi", lo, hi))
    store("yp", 0, 256, A("yv"))
    return ops


def overlap(a, b):
    if a[1] >= b[2] or b[1] >= a[2]:
        return False
    return not (a[3] == b[3] and a[3] > 1 and (a[1] - b[1]) % a[3])


def dependencies(ops):
    hist = {}
    for i, op in enumerate(ops):
        op["i"] = i
        deps = {}
        acc = [(a, False) for a in op["ins"]] + [(a, True) for a in op["outs"]]
        for a, wr in acc:
            for j, b, bw in hist.setdefault(a[0], []):
                same = ops[j]["q"] == op["q"]
                if (wr or bw) and overlap(a, b):
                    deps[j] = deps.get(j, False) or not same or op["q"] != "P"
                elif same and a[0] in PSUM and op["q"] == "P":
                    deps[j] = deps.get(j, False)
        for a, wr in acc:
            h = hist[a[0]]
            if a[0] in PSUM:
                h[:] = [e for e in h if e[0] >= i - 400]
            elif wr and a[3] == 1:
                h[:] = [e for e in h if not (e[0] != i and e[1][1] >= a[1] and e[1][2] <= a[2])]
            h.append((i, a, wr))
        op["deps"] = deps
        op["banks"] = {a[0] for a, _ in acc if a[0] in PSUM}


LOOK, BIG = 0.2, 0.45


def schedule(ops, wake=0.25):
    n = len(ops)
    succ = [[] for _ in range(n)]
    npred = [0] * n
    for i, op in enumerate(ops):
        op["preds"] = set(op["deps"]) | ({op["after"]["i"]} if "after" in op else set())
        npred[i] = len(op["preds"])
        for j in op["preds"]:
            succ[j].append(i)
    prio = [0.0] * n
    for i in range(n - 1, -1, -1):
        b = max([prio[k] + (0.0 if ops[k]["q"] == ops[i]["q"] else wake) for k in succ[i]] + [0.0])
        prio[i] = b + ops[i]["cost"] + ops[i].get("lat", 0.0)
    free, count, done, last = {}, {}, [0.0] * n, {}
    ready = {i for i in range(n) if npred[i] == 0}
    while ready:
        best = {}
        for i in sorted(ready):
            q = ops[i]["q"]
            s = free.get(q, 0.0) if q != "R" else 0.0
            for j in ops[i]["preds"]:
                s = max(s, done[j] + (wake if ops[j]["q"] != q else 0.02))
            for b in ops[i]["banks"]:
                for q2, j in last.get(b, {}).items():
                    if q2 != q:
                        s = max(s, done[j] + wake)
            best.setdefault(q, []).append((s, i))
        pick = None
        for q, lst in sorted(best.items()):
            m = min(s for s, _ in lst)
            s, i = max(((s, i) for s, i in lst if s <= m), key=lambda e: (prio[e[1]], -e[1]))
            if ops[i]["cost"] > BIG:
                s, i = max(((s, i) for s, i in lst if s <= m + LOOK), key=lambda e: (prio[e[1]], -e[1]))
            if pick is None or (s, -prio[i]) < pick[:2]:
                pick = (s, -prio[i], i, q)
        s, _, i, q = pick
        ready.remove(i)
        for b in ops[i]["banks"]:
            users = last.setdefault(b, {})
            for q2, j in users.items():
                if q2 != q:
                    ops[i]["deps"][j] = True
            users[q] = i
        free[q] = s + ops[i]["cost"]
        done[i] = s + ops[i]["cost"] + ops[i].get("lat", 0.0)
        count[q] = count.get(q, 0) + 1
        ops[i]["pos"] = (s, count[q])
        for k in succ[i]:
            npred[k] -= 1
            if npred[k] == 0:
                ready.add(k)


PLAN = {}


def plan():
    if not PLAN:
        ops = build()
        dependencies(ops)
        schedule(ops)
        PLAN["ops"], PLAN["seq"] = ops, sorted(range(len(ops)), key=lambda i: ops[i]["pos"])
    return PLAN["ops"], PLAN["seq"]


def rank_program(g, core, T, topo):
    rank = T.rank_of(core)
    if rank is None:
        return
    ops, seq = plan()
    ctx = dict(g=g, V=g.vector, S=g.scalar, P=g.tensor, T=T, topo=topo, core=core, rank=rank)
    queue = {"V": g.vector, "S": g.scalar, "P": g.tensor, "G": g, "Y": g.sync}
    default = {"V": "v", "S": "s", "P": "t"}
    total, val, known, clock = {}, {}, {q: {} for q in queue}, {}
    for i in seq:
        op = ops[i]
        q = op["q"]
        name = op.get("sem") or default[q]
        inc = op.get("inc", 1)
        if q == "R":
            total[name] = total.get(name, 0) + inc
            val[i], clock[i] = (name, total[name]), {name: total[name]}
            continue
        kn = known[q]
        hard = [j for j, h in op["deps"].items() if h]
        need = {}
        for j in hard:
            s, v = val[j]
            if kn.get(s, 0) < v:
                need[s] = max(need.get(s, 0), v)
        for j in sorted(hard, key=lambda j: -ops[j]["pos"][0]):
            s0, v0 = val[j]
            if need.get(s0) == v0:
                for s, v in clock[j].items():
                    if s != s0 and need.get(s, v + 1) <= v:
                        del need[s]
        for s in sorted(need):
            queue[q].wait_ge(T.sem[s], need[s])
        for j in hard:
            for s, v in clock[j].items():
                kn[s] = max(kn.get(s, 0), v)
        ins = op["fn"](ctx)
        total[name] = total.get(name, 0) + inc
        val[i] = (name, total[name])
        clock[i] = dict(kn)
        clock[i][name] = total[name]
        if not op.get("own"):
            ins.then_inc(T.sem[name], inc)
    for s in sorted(total):
        if known["G"].get(s, 0) < total[s]:
            g.wait_ge(T.sem[s], total[s])
